import numpy as np
import ml_dtypes


def mxq(x, axis, fmt="e4m3"):
    dtype, down = {"e4m3": (ml_dtypes.float8_e4m3fn, 7), "e5m2": (ml_dtypes.float8_e5m2, 14)}[fmt]
    v = np.moveaxis(np.asarray(x, np.float32).astype(ml_dtypes.bfloat16).astype(np.float64), axis, -1)
    blocks = v.reshape(v.shape[:-1] + (-1, 32))
    amax = np.abs(blocks).max(-1, keepdims=True)
    byte = np.maximum(np.where(amax > 0, np.frexp(amax)[1] - 1 + 127, 0) - down, 1)
    scale = np.exp2(byte - 127.0)
    codes = (blocks / scale).astype(np.float32).astype(dtype).astype(np.float64)
    return np.moveaxis((codes * scale).reshape(v.shape), -1, axis)


WIDE = False


def mx_kscale(k, group=512):
    if not WIDE:
        return np.ones(k)
    levels = np.array([10, -10, 5, -5, 0])
    if group != 512:
        return np.exp2(np.random.permutation(np.resize(levels, k // group))).repeat(group)
    if k % 512:
        return np.exp2(np.random.permutation(np.resize(levels, k // 32))).repeat(32)
    a = np.empty((k // 512, 16))
    for p in range(k // 512):
        a[p, :8] = np.random.permutation(np.resize(levels, 8))
        for g in range(8):
            far = levels[np.abs(levels - a[p, g]) >= 10]
            a[p, g + 8] = far[np.random.randint(len(far))]
    return np.exp2(a.ravel()).repeat(32)


def f64(x):
    return np.asarray(x).astype(np.float64)


G, D, M, N = 2, 256, 128, 512


def setup_inputs():
    n = np.random.standard_normal
    s_d = mx_kscale(D, 0)
    return {
        "x": (n((G, D, N)) * s_d[:, None]).astype(np.float32),
        "w1": (n((G, D, M)) / np.sqrt(D) / s_d[:, None]).astype(np.float32),
        "w2": (n((G, D, M)) / np.sqrt(D) / s_d[:, None]).astype(np.float32),
        "w3": (n((G, D, M)) / np.sqrt(D) / s_d[:, None]).astype(np.float32),
        "re": (np.random.uniform(0.3, 1.5, (G, M, 1))).astype(np.float32),
        "dx": (n((G, D, N)) * s_d[:, None]).astype(np.float32),
        "og": (np.random.uniform(0.5, 2.0, (G, M, 1))).astype(np.float32),
        "base": (0.3 * n((G, M, N))).astype(np.float32),
    }


def reference(x, w1, w2, w3, re, dx, og, base):
    w1q = mxq(f64(w1), 1, "e4m3")
    xq = mxq(f64(x), 1, "e4m3")
    z1 = w1q.transpose(0, 2, 1) @ xq
    dxq = mxq(f64(dx), 1, "e4m3")
    tz1 = w1q.transpose(0, 2, 1) @ dxq
    w2q = mxq(f64(w2), 1, "e4m3")
    z2 = w2q.transpose(0, 2, 1) @ xq
    tz2 = w2q.transpose(0, 2, 1) @ dxq
    w3q = mxq(f64(w3), 1, "e4m3")
    z3 = w3q.transpose(0, 2, 1) @ xq
    tz3 = w3q.transpose(0, 2, 1) @ dxq
    e1 = np.exp(z1)
    e2 = np.exp(z2)
    xe1 = tz1 * e1
    xe2 = tz2 * e2
    xh = (xe1 - (xe1 + xe2) * e1 / (e1 + e2 + f64(re))) / (e1 + e2 + f64(re)) * z3 + tz3 * e1 / (e1 + e2 + f64(re))
    y = xh * f64(og) + f64(base)
    return y

@@ -1,0 +1,175 @@
+from contextlib import ExitStack
+
+import concourse.mybir as mybir
+
+G, D, M, N = 2, 256, 128, 512
+FLOPS = 6 * 2 * G * D * M * N
+
+F32 = mybir.dt.float32
+BF16 = mybir.dt.bfloat16
+U32 = mybir.dt.uint32
+U8 = mybir.dt.uint8
+FP8X4 = mybir.dt.float8_e4m3fn_x4
+ACT = mybir.ActivationFunctionType
+ALU = mybir.AluOpType
+
+P = 128
+PACK = 4
+ROWS = D // PACK
+HALF = N // 2
+
+
+def tile_rows_tntwoshare_kernel(tc, x, w1, w2, w3, reserve, dx, og, base, out):
+    nc = tc.nc
+
+    with ExitStack() as ctx:
+        sb = ctx.enter_context(tc.tile_pool(name="sb", bufs=1))
+        ps = ctx.enter_context(tc.psum_pool(name="ps", bufs=1))
+        ctx.enter_context(tc.manual_schedule())
+
+        def load_rows(name, src, cols):
+            width = cols.stop - cols.start
+            raw = sb.tile([P, PACK, width], F32, name=name + "_raw", align_bytes=64)
+            nc.sync.dma_start(out=raw[:], in_=src.rearrange("g (p j) n -> (g p) j n", j=PACK)[:, :, cols])
+            return raw
+
+        def load_column(name, src):
+            col = sb.tile([P, G], F32, name=name)
+            with nc.allow_non_contiguous_dma(reason="one value a feature, features on partitions"):
+                nc.scalar.dma_start(out=col[:], in_=src.rearrange("g m o -> m (g o)"))
+            return col
+
+        def interleave(name, raw, copy):
+            width = raw.shape[2]
+            packed = sb.tile([P, width, PACK], BF16, name=name + "_bf", align_bytes=64)
+            copy(
+                out=packed[:].rearrange("p (c i) j -> p c j i", i=4),
+                in_=raw[:].rearrange("p j (c i) -> p c j i", i=4),
+            )
+            return packed
+
+        def planes(name, width):
+            codes = sb.tile([P, width], U32, name=name + "_codes", align_bytes=64)
+            scales = sb.tile([P, width], U8, name=name + "_scales", align_bytes=64)
+            return codes, scales
+
+        def quantize(operand, cols, packed):
+            codes, scales = operand
+            nc.vector.quantize_mx(
+                out=codes[:, cols].bitcast(FP8X4),
+                scales=scales[:, cols],
+                in_=packed[:].rearrange("p n j -> p (n j)"),
+            )
+
+        def product(bank, weights, moving, g):
+            rows = slice(ROWS * g, ROWS * (g + 1))
+            nc.tensor.matmul_mx(
+                out=bank[:],
+                lhsT=weights[0][rows, :].bitcast(FP8X4),
+                lhsT_scale=weights[1][rows, :],
+                rhs=moving[0][rows, :].bitcast(FP8X4),
+                rhs_scale=moving[1][rows, :],
+                start=True,
+                stop=True,
+            )
+
+        def work(name):
+            return [sb.tile([P, N], F32, name=name + str(g), align_bytes=64) for g in range(G)]
+
+        halves = [slice(0, HALF), slice(HALF, N)]
+        all_m = slice(0, M)
+        groups = range(G)
+
+        re_col = load_column("re_col", reserve)
+        x_raw = [load_rows("x" + str(h), x, halves[h]) for h in range(2)]
+        w2_raw = load_rows("w2", w2, all_m)
+        dx_raw = [load_rows("dx" + str(h), dx, halves[h]) for h in range(2)]
+        w1_raw = load_rows("w1", w1, all_m)
+        w3_raw = load_rows("w3", w3, all_m)
+        og_col = load_column("og_col", og)
+        base_sb = work("base")
+        for g in groups:
+            nc.sync.dma_start(out=base_sb[g][:], in_=base[g])
+
+        xq, dxq = planes("xq", N), planes("dxq", N)
+        w1q, w2q, w3q = planes("w1q", M), planes("w2q", M), planes("w3q", M)
+        banks = [[ps.tile([P, N], F32, name="bank" + str(g) + str(b)) for b in range(4)] for g in groups]
+        z2, tz2, tz1, z1 = ([banks[g][b] for g in groups] for b in range(4))
+        z3, tz3 = z2, tz2
+
+        ln_re = sb.tile([P, G], F32, name="ln_re")
+        warm = sb.tile([P, G], F32, name="warm")
+        nc.scalar.activation(out=ln_re[:], in_=re_col[:], func=ACT.Ln)
+        nc.scalar.activation(out=warm[:], in_=ln_re[:], func=ACT.Sigmoid)
+
+        x0_bf = interleave("x0", x_raw[0], nc.vector.tensor_copy)
+        quantize(xq, halves[0], x0_bf)
+        x1_bf = interleave("x1", x_raw[1], nc.vector.tensor_copy)
+        w2_bf = interleave("w2", w2_raw, nc.scalar.copy)
+        quantize(xq, halves[1], x1_bf)
+        quantize(w2q, all_m, w2_bf)
+        for g in groups:
+            product(z2[g], w2q, xq, g)
+
+        share = work("share")
+        for g in groups:
+            nc.scalar.activation(out=share[g][:], in_=z2[g][:], func=ACT.Sigmoid, bias=ln_re[:, g : g + 1], scale=-1.0)
+
+        dx0_bf = interleave("dx0", dx_raw[0], nc.vector.tensor_copy)
+        quantize(dxq, halves[0], dx0_bf)
+        dx1_bf = interleave("dx1", dx_raw[1], nc.vector.tensor_copy)
+        w1_bf = interleave("w1", w1_raw, nc.scalar.copy)
+        quantize(dxq, halves[1], dx1_bf)
+        for g in groups:
+            product(tz2[g], w2q, dxq, g)
+        w3_bf = interleave("w3", w3_raw, nc.vector.tensor_copy)
+        quantize(w1q, all_m, w1_bf)
+        quantize(w3q, all_m, w3_bf)
+        for g in groups:
+            product(tz1[g], w1q, dxq, g)
+        for g in groups:
+            product(z1[g], w1q, xq, g)
+        for g in groups:
+            product(z3[g], w3q, xq, g)
+
+        ln_share = work("ln_share")
+        for g in groups:
+            nc.scalar.activation(out=ln_share[g][:], in_=share[g][:], func=ACT.Ln)
+
+        mixed, slope, logit, gain = work("mixed"), work("slope"), work("logit"), work("gain")
+        for g in groups:
+            nc.vector.scalar_tensor_tensor(
+                out=mixed[g][:], in0=share[g][:], scalar=1.0, in1=tz2[g][:], op0=ALU.subtract, op1=ALU.mult
+            )
+        for g in groups:
+            product(tz3[g], w3q, dxq, g)
+        for g in groups:
+            nc.vector.tensor_tensor(out=slope[g][:], in0=mixed[g][:], in1=tz1[g][:], op=ALU.add)
+        for g in groups:
+            nc.vector.scalar_tensor_tensor(
+                out=logit[g][:], in0=ln_share[g][:], scalar=ln_re[:, g : g + 1], in1=z1[g][:],
+                op0=ALU.subtract, op1=ALU.add,
+            )
+        prob = work("prob")
+        for g in groups:
+            nc.scalar.activation(out=prob[g][:], in_=logit[g][:], func=ACT.Sigmoid)
+        for g in groups:
+            nc.vector.tensor_tensor(out=gain[g][:], in0=slope[g][:], in1=z3[g][:], op=ALU.mult)
+
+        damped, inner, scaled, result = work("damped"), work("inner"), work("scaled"), work("result")
+        for g in groups:
+            nc.vector.scalar_tensor_tensor(
+                out=damped[g][:], in0=prob[g][:], scalar=1.0, in1=gain[g][:], op0=ALU.subtract, op1=ALU.mult
+            )
+        for g in groups:
+            nc.vector.tensor_tensor(out=inner[g][:], in0=tz3[g][:], in1=damped[g][:], op=ALU.subtract)
+        for g in groups:
+            nc.vector.scalar_tensor_tensor(
+                out=scaled[g][:], in0=inner[g][:], scalar=og_col[:, g : g + 1], in1=prob[g][:],
+                op0=ALU.mult, op1=ALU.mult,
+            )
+        for g, cols, queue in ((0, slice(0, N), nc.sync), (1, halves[0], nc.scalar), (1, halves[1], nc.sync)):
+            nc.vector.tensor_tensor(
+                out=result[g][:, cols], in0=scaled[g][:, cols], in1=base_sb[g][:, cols], op=ALU.add
+            )
+            queue.dma_start(out=out[g][:, cols], in_=result[g][:, cols])

@@ -17,6 +17,7 @@ P = 128
 PACK = 4
 ROWS = D // PACK
 HALF = N // 2
+NT = 512
 
 
 def tile_rows_tntwoshare_kernel(tc, x, w1, w2, w3, reserve, dx, og, base, out):
@@ -33,10 +34,10 @@ def tile_rows_tntwoshare_kernel(tc, x, w1, w2, w3, reserve, dx, og, base, out):
             nc.sync.dma_start(out=raw[:], in_=src.rearrange("g (p j) n -> (g p) j n", j=PACK)[:, :, cols])
             return raw
 
-        def load_column(name, src):
+        def load_column(name, src, queue):
             col = sb.tile([P, G], F32, name=name)
             with nc.allow_non_contiguous_dma(reason="one value a feature, features on partitions"):
-                nc.scalar.dma_start(out=col[:], in_=src.rearrange("g m o -> m (g o)"))
+                queue.dma_start(out=col[:], in_=src.rearrange("g m o -> m (g o)"))
             return col
 
         def interleave(name, raw, copy):
@@ -44,7 +45,7 @@ def tile_rows_tntwoshare_kernel(tc, x, w1, w2, w3, reserve, dx, og, base, out):
             packed = sb.tile([P, width, PACK], BF16, name=name + "_bf", align_bytes=64)
             copy(
                 out=packed[:].rearrange("p (c i) j -> p c j i", i=4),
-                in_=raw[:].rearrange("p j (c i) -> p c j i", i=4),
+                in_=raw.rearrange("p j (c i) -> p c j i", i=4),
             )
             return packed
 
@@ -61,100 +62,91 @@ def tile_rows_tntwoshare_kernel(tc, x, w1, w2, w3, reserve, dx, og, base, out):
                 in_=packed[:].rearrange("p n j -> p (n j)"),
             )
 
-        def product(bank, weights, moving, g):
-            rows = slice(ROWS * g, ROWS * (g + 1))
-            nc.tensor.matmul_mx(
-                out=bank[:],
-                lhsT=weights[0][rows, :].bitcast(FP8X4),
-                lhsT_scale=weights[1][rows, :],
-                rhs=moving[0][rows, :].bitcast(FP8X4),
-                rhs_scale=moving[1][rows, :],
-                start=True,
-                stop=True,
-            )
+        def product(dst, weights, moving, cols):
+            for n0 in range(0, cols.stop - cols.start, NT):
+                for g in groups:
+                    rows = slice(ROWS * g, ROWS * (g + 1))
+                    part = slice(cols.start + n0, cols.start + n0 + NT)
+                    nc.tensor.matmul_mx(
+                        out=dst[g][:, n0 : n0 + NT],
+                        lhsT=weights[0][rows, :].bitcast(FP8X4),
+                        lhsT_scale=weights[1][rows, :],
+                        rhs=moving[0][rows, part].bitcast(FP8X4),
+                        rhs_scale=moving[1][rows, part],
+                        start=True,
+                        stop=True,
+                    )
 
         def work(name):
             return [sb.tile([P, N], F32, name=name + str(g), align_bytes=64) for g in range(G)]
 
         halves = [slice(0, HALF), slice(HALF, N)]
         all_m = slice(0, M)
+        all_n = slice(0, N)
         groups = range(G)
 
-        re_col = load_column("re_col", reserve)
-        x_raw = [load_rows("x" + str(h), x, halves[h]) for h in range(2)]
+        re_col = load_column("re_col", reserve, nc.scalar)
+        x0_raw = load_rows("x0", x, halves[0])
         w2_raw = load_rows("w2", w2, all_m)
+        x1_raw = load_rows("x1", x, halves[1])
         dx_raw = [load_rows("dx" + str(h), dx, halves[h]) for h in range(2)]
         w1_raw = load_rows("w1", w1, all_m)
         w3_raw = load_rows("w3", w3, all_m)
-        og_col = load_column("og_col", og)
         base_sb = work("base")
         for g in groups:
             nc.sync.dma_start(out=base_sb[g][:], in_=base[g])
+        og_col = load_column("og_col", og, nc.sync)
 
         xq, dxq = planes("xq", N), planes("dxq", N)
         w1q, w2q, w3q = planes("w1q", M), planes("w2q", M), planes("w3q", M)
         banks = [[ps.tile([P, N], F32, name="bank" + str(g) + str(b)) for b in range(4)] for g in groups]
-        z2, tz2, tz1, z1 = ([banks[g][b] for g in groups] for b in range(4))
+        z2, z1, tz2, tz1 = ([banks[g][b][:] for g in groups] for b in range(4))
         z3, tz3 = z2, tz2
 
         ln_re = sb.tile([P, G], F32, name="ln_re")
-        warm = sb.tile([P, G], F32, name="warm")
         nc.scalar.activation(out=ln_re[:], in_=re_col[:], func=ACT.Ln)
-        nc.scalar.activation(out=warm[:], in_=ln_re[:], func=ACT.Sigmoid)
 
-        x0_bf = interleave("x0", x_raw[0], nc.vector.tensor_copy)
-        quantize(xq, halves[0], x0_bf)
-        x1_bf = interleave("x1", x_raw[1], nc.vector.tensor_copy)
-        w2_bf = interleave("w2", w2_raw, nc.scalar.copy)
-        quantize(xq, halves[1], x1_bf)
-        quantize(w2q, all_m, w2_bf)
-        for g in groups:
-            product(z2[g], w2q, xq, g)
+        quantize(xq, halves[0], interleave("x0", x0_raw[:], nc.vector.tensor_copy))
+        quantize(w2q, all_m, interleave("w2", w2_raw[:], nc.vector.tensor_copy))
+        quantize(xq, halves[1], interleave("x1", x1_raw[:], nc.vector.tensor_copy))
+        product(z2, w2q, xq, all_n)
 
         share = work("share")
         for g in groups:
-            nc.scalar.activation(out=share[g][:], in_=z2[g][:], func=ACT.Sigmoid, bias=ln_re[:, g : g + 1], scale=-1.0)
+            nc.scalar.activation(out=share[g][:], in_=z2[g], func=ACT.Sigmoid, bias=ln_re[:, g : g + 1], scale=-1.0)
 
-        dx0_bf = interleave("dx0", dx_raw[0], nc.vector.tensor_copy)
-        quantize(dxq, halves[0], dx0_bf)
-        dx1_bf = interleave("dx1", dx_raw[1], nc.vector.tensor_copy)
-        w1_bf = interleave("w1", w1_raw, nc.scalar.copy)
-        quantize(dxq, halves[1], dx1_bf)
-        for g in groups:
-            product(tz2[g], w2q, dxq, g)
-        w3_bf = interleave("w3", w3_raw, nc.vector.tensor_copy)
-        quantize(w1q, all_m, w1_bf)
-        quantize(w3q, all_m, w3_bf)
-        for g in groups:
-            product(tz1[g], w1q, dxq, g)
-        for g in groups:
-            product(z1[g], w1q, xq, g)
-        for g in groups:
-            product(z3[g], w3q, xq, g)
+        for h in range(2):
+            quantize(dxq, halves[h], interleave("dx" + str(h), dx_raw[h][:], nc.vector.tensor_copy))
+        product(tz2, w2q, dxq, all_n)
+        quantize(w1q, all_m, interleave("w1", w1_raw[:], nc.vector.tensor_copy))
+        product(z1, w1q, xq, all_n)
+        product(tz1, w1q, dxq, all_n)
 
         ln_share = work("ln_share")
         for g in groups:
             nc.scalar.activation(out=ln_share[g][:], in_=share[g][:], func=ACT.Ln)
+        w3_bf = interleave("w3", w3_raw[:], nc.scalar.copy)
 
         mixed, slope, logit, gain = work("mixed"), work("slope"), work("logit"), work("gain")
         for g in groups:
             nc.vector.scalar_tensor_tensor(
-                out=mixed[g][:], in0=share[g][:], scalar=1.0, in1=tz2[g][:], op0=ALU.subtract, op1=ALU.mult
+                out=mixed[g][:], in0=share[g][:], scalar=1.0, in1=tz2[g], op0=ALU.subtract, op1=ALU.mult
             )
         for g in groups:
-            product(tz3[g], w3q, dxq, g)
-        for g in groups:
-            nc.vector.tensor_tensor(out=slope[g][:], in0=mixed[g][:], in1=tz1[g][:], op=ALU.add)
-        for g in groups:
             nc.vector.scalar_tensor_tensor(
-                out=logit[g][:], in0=ln_share[g][:], scalar=ln_re[:, g : g + 1], in1=z1[g][:],
+                out=logit[g][:], in0=ln_share[g][:], scalar=ln_re[:, g : g + 1], in1=z1[g],
                 op0=ALU.subtract, op1=ALU.add,
             )
         prob = work("prob")
         for g in groups:
             nc.scalar.activation(out=prob[g][:], in_=logit[g][:], func=ACT.Sigmoid)
+        quantize(w3q, all_m, w3_bf)
+        product(z3, w3q, xq, all_n)
+        product(tz3, w3q, dxq, all_n)
         for g in groups:
-            nc.vector.tensor_tensor(out=gain[g][:], in0=slope[g][:], in1=z3[g][:], op=ALU.mult)
+            nc.vector.tensor_tensor(out=slope[g][:], in0=mixed[g][:], in1=tz1[g], op=ALU.add)
+        for g in groups:
+            nc.vector.tensor_tensor(out=gain[g][:], in0=slope[g][:], in1=z3[g], op=ALU.mult)
 
         damped, inner, scaled, result = work("damped"), work("inner"), work("scaled"), work("result")
         for g in groups:
@@ -162,7 +154,7 @@ def tile_rows_tntwoshare_kernel(tc, x, w1, w2, w3, reserve, dx, og, base, out):
                 out=damped[g][:], in0=prob[g][:], scalar=1.0, in1=gain[g][:], op0=ALU.subtract, op1=ALU.mult
             )
         for g in groups:
-            nc.vector.tensor_tensor(out=inner[g][:], in0=tz3[g][:], in1=damped[g][:], op=ALU.subtract)
+            nc.vector.tensor_tensor(out=inner[g][:], in0=tz3[g], in1=damped[g][:], op=ALU.subtract)
         for g in groups:
             nc.vector.scalar_tensor_tensor(
                 out=scaled[g][:], in0=inner[g][:], scalar=og_col[:, g : g + 1], in1=prob[g][:],

@@ -18,6 +18,8 @@ PACK = 4
 ROWS = D // PACK
 HALF = N // 2
 NT = 512
+SHARE = 128
+QUAD = 32
 
 
 def tile_rows_tntwoshare_kernel(tc, x, w1, w2, w3, reserve, dx, og, base, out):
@@ -34,19 +36,15 @@ def tile_rows_tntwoshare_kernel(tc, x, w1, w2, w3, reserve, dx, og, base, out):
             nc.sync.dma_start(out=raw[:], in_=src.rearrange("g (p j) n -> (g p) j n", j=PACK)[:, :, cols])
             return raw
 
-        def load_column(name, src, queue):
-            col = sb.tile([P, G], F32, name=name)
-            with nc.allow_non_contiguous_dma(reason="one value a feature, features on partitions"):
-                queue.dma_start(out=col[:], in_=src.rearrange("g m o -> m (g o)"))
-            return col
-
-        def interleave(name, raw, copy):
-            width = raw.shape[2]
-            packed = sb.tile([P, width, PACK], BF16, name=name + "_bf", align_bytes=64)
+        def interleave_into(packed, raw, copy):
             copy(
-                out=packed[:].rearrange("p (c i) j -> p c j i", i=4),
+                out=packed.rearrange("p (c i) j -> p c j i", i=4),
                 in_=raw.rearrange("p j (c i) -> p c j i", i=4),
             )
+
+        def interleave(name, raw, copy):
+            packed = sb.tile([P, raw.shape[2], PACK], BF16, name=name + "_bf", align_bytes=64)
+            interleave_into(packed[:], raw, copy)
             return packed
 
         def planes(name, width):
@@ -85,17 +83,23 @@ def tile_rows_tntwoshare_kernel(tc, x, w1, w2, w3, reserve, dx, og, base, out):
         all_n = slice(0, N)
         groups = range(G)
 
-        re_col = load_column("re_col", reserve, nc.scalar)
-        x0_raw = load_rows("x0", x, halves[0])
+        rows = sb.tile([P, P], F32, name="rows", align_bytes=64)
+        nc.vector.memset(rows[:], 0.0)
         w2_raw = load_rows("w2", w2, all_m)
-        x1_raw = load_rows("x1", x, halves[1])
-        dx_raw = [load_rows("dx" + str(h), dx, halves[h]) for h in range(2)]
+        for slot, src in enumerate((reserve, og)):
+            nc.sync.dma_start(
+                out=rows[0:P:QUAD, G * QUAD * slot : G * QUAD * (slot + 1)].rearrange("q (g c) -> q g c", g=G),
+                in_=src.rearrange("g (q c) o -> q g (c o)", c=QUAD),
+            )
+        x_raw = load_rows("x", x, all_n)
+        dx_raw = load_rows("dx", dx, all_n)
         w1_raw = load_rows("w1", w1, all_m)
         w3_raw = load_rows("w3", w3, all_m)
         base_sb = work("base")
         for g in groups:
             nc.sync.dma_start(out=base_sb[g][:], in_=base[g])
-        og_col = load_column("og_col", og, nc.sync)
+        columns = sb.tile([P, P], F32, name="columns", align_bytes=64)
+        nc.vector.transpose(columns[:], rows[:])
 
         xq, dxq = planes("xq", N), planes("dxq", N)
         w1q, w2q, w3q = planes("w1q", M), planes("w2q", M), planes("w3q", M)
@@ -104,34 +108,49 @@ def tile_rows_tntwoshare_kernel(tc, x, w1, w2, w3, reserve, dx, og, base, out):
         z3, tz3 = z2, tz2
 
         ln_re = sb.tile([P, G], F32, name="ln_re")
-        nc.scalar.activation(out=ln_re[:], in_=re_col[:], func=ACT.Ln)
+        nc.scalar.activation(out=ln_re[:], in_=columns[:, 0 : G * QUAD : QUAD], func=ACT.Ln)
+        warm = sb.tile([P, G], F32, name="warm")
+        nc.scalar.activation(out=warm[:], in_=ln_re[:], func=ACT.Sigmoid)
 
-        quantize(xq, halves[0], interleave("x0", x0_raw[:], nc.vector.tensor_copy))
         quantize(w2q, all_m, interleave("w2", w2_raw[:], nc.vector.tensor_copy))
-        quantize(xq, halves[1], interleave("x1", x1_raw[:], nc.vector.tensor_copy))
+        x0_bf = interleave("x0", x_raw[:, :, halves[0]], nc.vector.tensor_copy)
+        x1_bf = sb.tile([P, HALF, PACK], BF16, name="x1_bf", align_bytes=64)
+        interleave_into(x1_bf[:, :SHARE, :], x_raw[:, :, HALF : HALF + SHARE], nc.vector.tensor_copy)
+        interleave_into(x1_bf[:, SHARE:, :], x_raw[:, :, HALF + SHARE :], nc.scalar.copy)
+        quantize(xq, halves[0], x0_bf)
+        quantize(xq, halves[1], x1_bf)
         product(z2, w2q, xq, all_n)
 
         share = work("share")
         for g in groups:
             nc.scalar.activation(out=share[g][:], in_=z2[g], func=ACT.Sigmoid, bias=ln_re[:, g : g + 1], scale=-1.0)
 
+        dx_bf = [interleave("dx" + str(h), dx_raw[:, :, halves[h]], nc.vector.tensor_copy) for h in range(2)]
         for h in range(2):
-            quantize(dxq, halves[h], interleave("dx" + str(h), dx_raw[h][:], nc.vector.tensor_copy))
+            quantize(dxq, halves[h], dx_bf[h])
         product(tz2, w2q, dxq, all_n)
-        quantize(w1q, all_m, interleave("w1", w1_raw[:], nc.vector.tensor_copy))
-        product(z1, w1q, xq, all_n)
+        w1_bf = interleave("w1", w1_raw[:], nc.vector.tensor_copy)
+        w3_bf = interleave("w3", w3_raw[:], nc.vector.tensor_copy)
+        quantize(w1q, all_m, w1_bf)
+        quantize(w3q, all_m, w3_bf)
         product(tz1, w1q, dxq, all_n)
+        product(z1, w1q, xq, all_n)
+        product(z3, w3q, xq, all_n)
 
         ln_share = work("ln_share")
         for g in groups:
             nc.scalar.activation(out=ln_share[g][:], in_=share[g][:], func=ACT.Ln)
-        w3_bf = interleave("w3", w3_raw[:], nc.scalar.copy)
+        warm2 = sb.tile([P, G], F32, name="warm2")
+        nc.scalar.activation(out=warm2[:], in_=ln_re[:], func=ACT.Sigmoid)
 
         mixed, slope, logit, gain = work("mixed"), work("slope"), work("logit"), work("gain")
         for g in groups:
             nc.vector.scalar_tensor_tensor(
                 out=mixed[g][:], in0=share[g][:], scalar=1.0, in1=tz2[g], op0=ALU.subtract, op1=ALU.mult
             )
+        product(tz3, w3q, dxq, all_n)
+        for g in groups:
+            nc.vector.tensor_tensor(out=slope[g][:], in0=mixed[g][:], in1=tz1[g], op=ALU.add)
         for g in groups:
             nc.vector.scalar_tensor_tensor(
                 out=logit[g][:], in0=ln_share[g][:], scalar=ln_re[:, g : g + 1], in1=z1[g],
@@ -140,11 +159,6 @@ def tile_rows_tntwoshare_kernel(tc, x, w1, w2, w3, reserve, dx, og, base, out):
         prob = work("prob")
         for g in groups:
             nc.scalar.activation(out=prob[g][:], in_=logit[g][:], func=ACT.Sigmoid)
-        quantize(w3q, all_m, w3_bf)
-        product(z3, w3q, xq, all_n)
-        product(tz3, w3q, dxq, all_n)
-        for g in groups:
-            nc.vector.tensor_tensor(out=slope[g][:], in0=mixed[g][:], in1=tz1[g], op=ALU.add)
         for g in groups:
             nc.vector.tensor_tensor(out=gain[g][:], in0=slope[g][:], in1=z3[g], op=ALU.mult)
 
@@ -157,7 +171,7 @@ def tile_rows_tntwoshare_kernel(tc, x, w1, w2, w3, reserve, dx, og, base, out):
             nc.vector.tensor_tensor(out=inner[g][:], in0=tz3[g], in1=damped[g][:], op=ALU.subtract)
         for g in groups:
             nc.vector.scalar_tensor_tensor(
-                out=scaled[g][:], in0=inner[g][:], scalar=og_col[:, g : g + 1], in1=prob[g][:],
+                out=scaled[g][:], in0=inner[g][:], scalar=columns[:, (G + g) * QUAD : (G + g) * QUAD + 1], in1=prob[g][:],
                 op0=ALU.mult, op1=ALU.mult,
             )
         for g, cols, queue in ((0, slice(0, N), nc.sync), (1, halves[0], nc.scalar), (1, halves[1], nc.sync)):

from contextlib import ExitStack

import concourse.mybir as mybir

G, D, M, N = 2, 256, 128, 512
FLOPS = 6 * 2 * G * D * M * N

F32 = mybir.dt.float32
BF16 = mybir.dt.bfloat16
U32 = mybir.dt.uint32
U8 = mybir.dt.uint8
FP8X4 = mybir.dt.float8_e4m3fn_x4
ACT = mybir.ActivationFunctionType
ALU = mybir.AluOpType

P = 128
PACK = 4
ROWS = D // PACK
HALF = N // 2
NT = 512
SHARE = 128
QUAD = 32


def tile_rows_tntwoshare_kernel(tc, x, w1, w2, w3, reserve, dx, og, base, out):
    nc = tc.nc

    with ExitStack() as ctx:
        sb = ctx.enter_context(tc.tile_pool(name="sb", bufs=1))
        ps = ctx.enter_context(tc.psum_pool(name="ps", bufs=1))
        ctx.enter_context(tc.manual_schedule())

        def load_rows(name, src, cols):
            width = cols.stop - cols.start
            raw = sb.tile([P, PACK, width], F32, name=name + "_raw", align_bytes=64)
            nc.sync.dma_start(out=raw[:], in_=src.rearrange("g (p j) n -> (g p) j n", j=PACK)[:, :, cols])
            return raw

        def interleave_into(packed, raw, copy):
            copy(
                out=packed.rearrange("p (c i) j -> p c j i", i=4),
                in_=raw.rearrange("p j (c i) -> p c j i", i=4),
            )

        def interleave(name, raw, copy):
            packed = sb.tile([P, raw.shape[2], PACK], BF16, name=name + "_bf", align_bytes=64)
            interleave_into(packed[:], raw, copy)
            return packed

        def planes(name, width):
            codes = sb.tile([P, width], U32, name=name + "_codes", align_bytes=64)
            scales = sb.tile([P, width], U8, name=name + "_scales", align_bytes=64)
            return codes, scales

        def quantize(operand, cols, packed):
            codes, scales = operand
            nc.vector.quantize_mx(
                out=codes[:, cols].bitcast(FP8X4),
                scales=scales[:, cols],
                in_=packed[:].rearrange("p n j -> p (n j)"),
            )

        def product(dst, weights, moving, cols):
            for n0 in range(0, cols.stop - cols.start, NT):
                for g in groups:
                    rows = slice(ROWS * g, ROWS * (g + 1))
                    part = slice(cols.start + n0, cols.start + n0 + NT)
                    nc.tensor.matmul_mx(
                        out=dst[g][:, n0 : n0 + NT],
                        lhsT=weights[0][rows, :].bitcast(FP8X4),
                        lhsT_scale=weights[1][rows, :],
                        rhs=moving[0][rows, part].bitcast(FP8X4),
                        rhs_scale=moving[1][rows, part],
                        start=True,
                        stop=True,
                    )

        def work(name):
            return [sb.tile([P, N], F32, name=name + str(g), align_bytes=64) for g in range(G)]

        halves = [slice(0, HALF), slice(HALF, N)]
        all_m = slice(0, M)
        all_n = slice(0, N)
        groups = range(G)

        rows = sb.tile([P, P], F32, name="rows", align_bytes=64)
        nc.vector.memset(rows[:], 0.0)
        w2_raw = load_rows("w2", w2, all_m)
        for slot, src in enumerate((reserve, og)):
            nc.sync.dma_start(
                out=rows[0:P:QUAD, G * QUAD * slot : G * QUAD * (slot + 1)].rearrange("q (g c) -> q g c", g=G),
                in_=src.rearrange("g (q c) o -> q g (c o)", c=QUAD),
            )
        x_raw = load_rows("x", x, all_n)
        dx_raw = load_rows("dx", dx, all_n)
        w1_raw = load_rows("w1", w1, all_m)
        w3_raw = load_rows("w3", w3, all_m)
        base_sb = work("base")
        for g in groups:
            nc.sync.dma_start(out=base_sb[g][:], in_=base[g])
        columns = sb.tile([P, P], F32, name="columns", align_bytes=64)
        nc.vector.transpose(columns[:], rows[:])

        xq, dxq = planes("xq", N), planes("dxq", N)
        w1q, w2q, w3q = planes("w1q", M), planes("w2q", M), planes("w3q", M)
        banks = [[ps.tile([P, N], F32, name="bank" + str(g) + str(b)) for b in range(4)] for g in groups]
        z2, z1, tz2, tz1 = ([banks[g][b][:] for g in groups] for b in range(4))
        z3, tz3 = z2, tz2

        ln_re = sb.tile([P, G], F32, name="ln_re")
        nc.scalar.activation(out=ln_re[:], in_=columns[:, 0 : G * QUAD : QUAD], func=ACT.Ln)
        warm = sb.tile([P, G], F32, name="warm")
        nc.scalar.activation(out=warm[:], in_=ln_re[:], func=ACT.Sigmoid)

        quantize(w2q, all_m, interleave("w2", w2_raw[:], nc.vector.tensor_copy))
        x0_bf = interleave("x0", x_raw[:, :, halves[0]], nc.vector.tensor_copy)
        x1_bf = sb.tile([P, HALF, PACK], BF16, name="x1_bf", align_bytes=64)
        interleave_into(x1_bf[:, :SHARE, :], x_raw[:, :, HALF : HALF + SHARE], nc.vector.tensor_copy)
        interleave_into(x1_bf[:, SHARE:, :], x_raw[:, :, HALF + SHARE :], nc.scalar.copy)
        quantize(xq, halves[0], x0_bf)
        quantize(xq, halves[1], x1_bf)
        product(z2, w2q, xq, all_n)

        share = work("share")
        for g in groups:
            nc.scalar.activation(out=share[g][:], in_=z2[g], func=ACT.Sigmoid, bias=ln_re[:, g : g + 1], scale=-1.0)

        dx_bf = [interleave("dx" + str(h), dx_raw[:, :, halves[h]], nc.vector.tensor_copy) for h in range(2)]
        for h in range(2):
            quantize(dxq, halves[h], dx_bf[h])
        product(tz2, w2q, dxq, all_n)
        w1_bf = interleave("w1", w1_raw[:], nc.vector.tensor_copy)
        w3_bf = interleave("w3", w3_raw[:], nc.vector.tensor_copy)
        quantize(w1q, all_m, w1_bf)
        quantize(w3q, all_m, w3_bf)
        product(tz1, w1q, dxq, all_n)
        product(z1, w1q, xq, all_n)
        product(z3, w3q, xq, all_n)

        ln_share = work("ln_share")
        for g in groups:
            nc.scalar.activation(out=ln_share[g][:], in_=share[g][:], func=ACT.Ln)
        warm2 = sb.tile([P, G], F32, name="warm2")
        nc.scalar.activation(out=warm2[:], in_=ln_re[:], func=ACT.Sigmoid)

        mixed, slope, logit, gain = work("mixed"), work("slope"), work("logit"), work("gain")
        for g in groups:
            nc.vector.scalar_tensor_tensor(
                out=mixed[g][:], in0=share[g][:], scalar=1.0, in1=tz2[g], op0=ALU.subtract, op1=ALU.mult
            )
        product(tz3, w3q, dxq, all_n)
        for g in groups:
            nc.vector.tensor_tensor(out=slope[g][:], in0=mixed[g][:], in1=tz1[g], op=ALU.add)
        for g in groups:
            nc.vector.scalar_tensor_tensor(
                out=logit[g][:], in0=ln_share[g][:], scalar=ln_re[:, g : g + 1], in1=z1[g],
                op0=ALU.subtract, op1=ALU.add,
            )
        prob = work("prob")
        for g in groups:
            nc.scalar.activation(out=prob[g][:], in_=logit[g][:], func=ACT.Sigmoid)
        for g in groups:
            nc.vector.tensor_tensor(out=gain[g][:], in0=slope[g][:], in1=z3[g], op=ALU.mult)

        damped, inner, scaled, result = work("damped"), work("inner"), work("scaled"), work("result")
        for g in groups:
            nc.vector.scalar_tensor_tensor(
                out=damped[g][:], in0=prob[g][:], scalar=1.0, in1=gain[g][:], op0=ALU.subtract, op1=ALU.mult
            )
        for g in groups:
            nc.vector.tensor_tensor(out=inner[g][:], in0=tz3[g], in1=damped[g][:], op=ALU.subtract)
        for g in groups:
            nc.vector.scalar_tensor_tensor(
                out=scaled[g][:], in0=inner[g][:], scalar=columns[:, (G + g) * QUAD : (G + g) * QUAD + 1], in1=prob[g][:],
                op0=ALU.mult, op1=ALU.mult,
            )
        for g, cols, queue in ((0, slice(0, N), nc.sync), (1, halves[0], nc.scalar), (1, halves[1], nc.sync)):
            nc.vector.tensor_tensor(
                out=result[g][:, cols], in0=scaled[g][:, cols], in1=base_sb[g][:, cols], op=ALU.add
            )
            queue.dma_start(out=out[g][:, cols], in_=result[g][:, cols])
